import numpy as np
import ml_dtypes


def mxq(x, axis, fmt="e4m3"):
    dtype, down = {"e4m3": (ml_dtypes.float8_e4m3fn, 7), "e5m2": (ml_dtypes.float8_e5m2, 14)}[fmt]
    v = np.moveaxis(np.asarray(x, np.float32).astype(ml_dtypes.bfloat16).astype(np.float64), axis, -1)
    blocks = v.reshape(v.shape[:-1] + (-1, 32))
    amax = np.abs(blocks).max(-1, keepdims=True)
    byte = np.maximum(np.where(amax > 0, np.frexp(amax)[1] - 1 + 127, 0) - down, 1)
    scale = np.exp2(byte - 127.0)
    codes = (blocks / scale).astype(np.float32).astype(dtype).astype(np.float64)
    return np.moveaxis((codes * scale).reshape(v.shape), -1, axis)


WIDE = False


def mx_kscale(k):
    if not WIDE:
        return np.ones(k)
    levels = np.array([24, -24, 12, -12, 0])
    if k % 512:
        return np.exp2(np.random.permutation(np.resize(levels, k // 32))).repeat(32)
    a = np.empty((k // 512, 16))
    for p in range(k // 512):
        a[p, :8] = np.random.permutation(np.resize(levels, 8))
        for g in range(8):
            far = levels[np.abs(levels - a[p, g]) >= 10]
            a[p, g + 8] = far[np.random.randint(len(far))]
    return np.exp2(a.ravel()).repeat(32)


def f64(x):
    return np.asarray(x).astype(np.float64)


def striped8(idx):
    return np.concatenate([v.reshape(-1, 16).T for v in idx]).astype(np.uint16)


def unstriped8(offs):
    return np.stack([offs[16 * g:16 * g + 16].T.reshape(-1) for g in range(8)]).astype(np.int64)


E2M1 = np.array([0.0, 0.5, 1.0, 1.5, 2.0, 3.0, 4.0, 6.0, -0.0, -0.5, -1.0, -1.5, -2.0, -3.0, -4.0, -6.0])


def pack_weight(w, fmt):
    k, n = w.shape
    w = f64(np.asarray(w, np.float32).astype(ml_dtypes.bfloat16)).reshape(k // 32, 32, n)
    amax = np.abs(w).max(1)
    if fmt == "e4m3":
        byte = np.frexp(amax)[1] - 1 + 127 - 7
    else:
        mant, ex = np.frexp(amax / 6.0)
        byte = np.where(mant > 0.5, ex, ex - 1) + 127
    byte = np.clip(np.where(amax > 0, byte, 1), 1, 254)
    scaled = (w * np.exp2(127.0 - byte)[:, None, :]).reshape(k, n).astype(np.float32)
    by_word = np.ascontiguousarray(scaled.reshape(k // 512, 128, 4, n).transpose(0, 1, 3, 2))
    if fmt == "e4m3":
        words = by_word.astype(ml_dtypes.float8_e4m3fn).view(np.uint8)
    else:
        c = by_word.astype(ml_dtypes.float4_e2m1fn).view(np.uint8) & 0xF
        words = (c[..., 0::2] | (c[..., 1::2] << 4)).reshape(k // 512, 128, 2 * n)
    return np.ascontiguousarray(words), np.ascontiguousarray(byte.astype(np.uint8).reshape(k // 512, 16, n))


def unpack_weight(words, scales, fmt):
    g, _, n = scales.shape
    words = np.ascontiguousarray(words).reshape(g, 128, n, -1)
    if fmt == "e4m3":
        vals = words.view(ml_dtypes.float8_e4m3fn).astype(np.float64)
    else:
        nib = np.empty((g, 128, n, 4), np.uint8)
        nib[..., 0::2] = words & 0xF
        nib[..., 1::2] = words >> 4
        vals = E2M1[nib]
    vals = vals * np.repeat(np.exp2(scales.astype(np.float64) - 127.0), 8, axis=1)[..., None]
    return vals.transpose(0, 1, 3, 2).reshape(g * 512, n)


K, L, N, T, J = 512, 512, 512, 2048, 1024


def setup_inputs():
    n = np.random.standard_normal
    s = mx_kscale(K)[:, None]
    s2 = mx_kscale(L)[:, None]
    p_wa = pack_weight(n((K, N)) / np.sqrt(K) / s, "e2m1")
    return {
        "xT": (n((K, T)) * s).astype(np.float32),
        "wgt": np.repeat(np.random.uniform(0.5, 2.0, (8, J)), 16, axis=0).astype(np.float32),
        "zT": (n((L, T)) * s2).astype(np.float32),
        "wgt2": np.repeat(np.random.uniform(0.5, 2.0, (8, J)), 16, axis=0).astype(np.float32),
        "wa_words": p_wa[0],
        "wa_scales": p_wa[1],
        "wb": (n((L, N)) / np.sqrt(L) / s2).astype(np.float32),
        "b": (0.3 * n(N)).astype(np.float32),
        "offs": striped8(np.stack([np.random.permutation(T)[:J] for _ in range(8)])),
        "offs2": striped8(np.stack([np.random.permutation(T)[:J] for _ in range(8)])),
    }


def reference(xT, wgt, zT, wgt2, wa_words, wa_scales, wb, b, offs, offs2):
    idx = unstriped8(offs)
    idx2 = unstriped8(offs2)
    rows = np.arange(K)
    xg = f64(wgt)[rows // 4 % 128] * f64(xT)[rows[:, None], idx[rows % 512 // 64]]
    xT_ = mxq(xg, 0, "e4m3")
    rows = np.arange(L)
    xg = f64(wgt2)[rows // 4 % 128] * f64(zT)[rows[:, None], idx2[rows % 512 // 64]]
    zT_ = mxq(xg, 0, "e4m3")
    wa_ = unpack_weight(wa_words, wa_scales, "e2m1")
    wb_ = mxq(f64(wb), 0, "e4m3")
    ya = wa_.T @ xT_
    yb = wb_.T @ zT_
    return ya * yb + f64(b)[:, None]

@@ -1,0 +1,207 @@
+from contextlib import ExitStack
+
+import concourse.mybir as mybir
+from concourse.masks import make_identity
+
+K, L, N, T, J = 512, 512, 512, 2048, 1024
+FLOPS = 2 * (K + L) * N * J
+
+F32 = mybir.dt.float32
+BF16 = mybir.dt.bfloat16
+I32 = mybir.dt.int32
+U32 = mybir.dt.uint32
+U16 = mybir.dt.uint16
+U8 = mybir.dt.uint8
+FP8X4 = mybir.dt.float8_e4m3fn_x4
+FP4X4 = mybir.dt.float4_e2m1fn_x4
+MULT = mybir.AluOpType.mult
+IDENTITY = mybir.ActivationFunctionType.Identity
+
+P = 128
+PACK = 4
+GROUP = 16
+NT = N // P
+BANK = 512
+X_SLICE = 512
+Z_SLICE = 256
+W_HALF = J // 2
+
+
+def interleave(engine_copy, dst, src):
+    engine_copy(
+        dst.rearrange("p (c i) t -> p c t i", i=4),
+        src.rearrange("p t (c i) -> p c t i", i=4),
+    )
+
+
+def tile_list_mul_bias_kernel(
+    tc, xT, wgt, zT, wgt2, wa_words, wa_scales, wb, b, offs, offs2, out
+):
+    nc = tc.nc
+    with ExitStack() as ctx:
+        keep = ctx.enter_context(tc.tile_pool(name="keep", bufs=1))
+        psum = ctx.enter_context(tc.psum_pool(name="psum", bufs=1))
+
+        x_list = keep.tile([P, J // GROUP], U16, name="x_list")
+        z_list = keep.tile([P, J // GROUP], U16, name="z_list")
+        x_planes = [keep.tile([P, T], F32, name=f"x_plane{i}") for i in range(PACK)]
+        z_planes = [keep.tile([P, T], F32, name=f"z_plane{i}", align_bytes=64) for i in range(PACK)]
+        x_wgt = [keep.tile([P, W_HALF], F32, name=f"x_wgt{h}") for h in range(2)]
+        z_wgt = [keep.tile([P, W_HALF], F32, name=f"z_wgt{h}") for h in range(2)]
+        wa_codes = keep.tile([P, 2 * N], U8, name="wa_codes", align_bytes=64)
+        wa_scale = keep.tile([P, N], U8, name="wa_scale", align_bytes=64)
+        wb_raw = [keep.tile([P, PACK, N // 2], F32, name=f"wb_raw{h}") for h in range(2)]
+        b_rows = keep.tile([P, P], F32, name="b_rows")
+        ident = keep.tile([P, P], F32, name="ident")
+        bias = keep.tile([P, NT], F32, name="bias")
+        banks = [psum.tile([P, BANK], F32, name=f"bank{i}") for i in range(8)]
+
+        xT_planes = xT.rearrange("(p i) t -> i p t", i=PACK)
+        zT_planes = zT.rearrange("(p i) t -> i p t", i=PACK)
+
+        make_identity(nc, ident[:])
+        nc.vector.memset(b_rows[:], 0.0)
+        nc.vector.memset(wa_scale[:].bitcast(I32), 0)
+
+        def load_scale_rows(q):
+            nc.sync.dma_start(
+                wa_scale[32 * q : 32 * q + 4, :].bitcast(I32),
+                wa_scales[0, 4 * q : 4 * q + 4, :].bitcast(I32),
+            )
+
+        nc.sync.dma_start(x_planes[0][:], xT_planes[0])
+        nc.sync.dma_start(x_list[:], offs)
+        for h in range(2):
+            nc.sync.dma_start(x_wgt[h][:], wgt[:, h * W_HALF : (h + 1) * W_HALF])
+        nc.sync.dma_start(b_rows[0:NT, :], b.rearrange("(t c) -> t c", c=P))
+        nc.sync.dma_start(x_planes[1][:], xT_planes[1])
+        load_scale_rows(0)
+        load_scale_rows(1)
+        nc.sync.dma_start(x_planes[2][:], xT_planes[2])
+        load_scale_rows(2)
+        load_scale_rows(3)
+        nc.sync.dma_start(x_planes[3][:], xT_planes[3])
+        nc.sync.dma_start(wa_codes[:].bitcast(I32), wa_words[0].bitcast(I32))
+        nc.sync.dma_start(z_list[:], offs2)
+        nc.sync.dma_start(z_wgt[0][:], wgt2[:, 0:W_HALF])
+        nc.sync.dma_start(z_planes[0][:], zT_planes[0])
+        nc.sync.dma_start(z_wgt[1][:], wgt2[:, W_HALF:J])
+        wb_rows = wb.rearrange("(p i) n -> p i n", i=PACK)
+        nc.sync.dma_start(z_planes[1][:], zT_planes[1])
+        nc.sync.dma_start(wb_raw[0][:], wb_rows[:, :, 0 : N // 2])
+        nc.sync.dma_start(z_planes[2][:], zT_planes[2])
+        nc.sync.dma_start(wb_raw[1][:], wb_rows[:, :, N // 2 : N])
+        nc.sync.dma_start(z_planes[3][:], zT_planes[3])
+
+        nc.tensor.transpose(banks[7][:, 0:P], b_rows[:], ident[:])
+        nc.scalar.activation(bias[:], banks[7][:, 0:NT], IDENTITY)
+
+        def gather(dst, plane, lst, weights, j0, width):
+            nc.vector.tensor_tensor(
+                dst,
+                plane[:].indirect(lst[:, j0 // GROUP : (j0 + width) // GROUP]),
+                weights[j0 // W_HALF][:, j0 % W_HALF : j0 % W_HALF + width],
+                MULT,
+            )
+
+        def quantize(name, src, width, tag=None):
+            codes = keep.tile([P, width], U32, name=name + "_codes", tag=tag or name + "_codes", align_bytes=64)
+            scale = keep.tile([P, width], U8, name=name + "_scale", align_bytes=64)
+            nc.vector.quantize_mx(
+                out=codes[:].bitcast(FP8X4),
+                scales=scale[:],
+                in_=src[:].rearrange("p w t -> p (w t)"),
+            )
+            return codes, scale
+
+        xs = J // X_SLICE
+        zs = J // Z_SLICE
+        per = X_SLICE // Z_SLICE
+        xg = [keep.tile([P, PACK, X_SLICE], F32, name=f"xg{s}") for s in range(xs)]
+        xb = [keep.tile([P, X_SLICE, PACK], BF16, name=f"xb{s}", align_bytes=64) for s in range(xs)]
+        zg = keep.tile([P, PACK, J], F32, name="zg")
+        zb = [keep.tile([P, Z_SLICE, PACK], BF16, name=f"zb{s}", align_bytes=64) for s in range(zs)]
+        ya = []
+        wbb = [keep.tile([P, N // 2, PACK], BF16, name=f"wbb{h}", align_bytes=64) for h in range(2)]
+        out_tiles = out.rearrange("(t p) j -> p t j", p=P)
+
+        def gather_z(i, width):
+            for j0 in range(0, J, width):
+                gather(zg[:, i, j0 : j0 + width], z_planes[i], z_list, z_wgt, j0, width)
+
+        def project_x(s):
+            codes, scale = quantize(f"xq{s}", xb[s], X_SLICE, tag=f"z_plane{s}")
+            for t in range(NT):
+                nc.tensor.matmul_mx(
+                    out=banks[s * NT + t][:],
+                    lhsT=wa_codes[:, 2 * P * t : 2 * P * (t + 1)].bitcast(FP4X4),
+                    lhsT_scale=wa_scale[:, P * t : P * (t + 1)],
+                    rhs=codes[:].bitcast(FP8X4),
+                    rhs_scale=scale[:],
+                    start=True,
+                    stop=True,
+                )
+
+        def keep_ya(s):
+            ya.append(keep.tile([P, per, NT, Z_SLICE], F32, name=f"ya{s}", tag="wb_raw1" if s else "ya0"))
+            for t in range(NT):
+                nc.scalar.copy(
+                    ya[s][:, :, t, :],
+                    banks[s * NT + t][:].rearrange("p (s j) -> p s j", s=per),
+                )
+
+        def finish(s, codes, scale):
+            prod = keep.tile([P, NT, Z_SLICE], F32, name=f"prod{s}")
+            res = keep.tile([P, NT, Z_SLICE], F32, name=f"res{s}")
+            for u in range(NT // 2):
+                bank = banks[2 * s + u]
+                for v in range(2):
+                    t = 2 * u + v
+                    nc.tensor.matmul_mx(
+                        out=bank[:, v * Z_SLICE : (v + 1) * Z_SLICE],
+                        lhsT=wq[u][0][:, P * v : P * (v + 1)].bitcast(FP8X4),
+                        lhsT_scale=wq[u][1][:, P * v : P * (v + 1)],
+                        rhs=codes[:].bitcast(FP8X4),
+                        rhs_scale=scale[:],
+                        start=True,
+                        stop=True,
+                    )
+                nc.vector.tensor_tensor(
+                    prod[:, 2 * u : 2 * u + 2, :].rearrange("p t j -> p (t j)"),
+                    bank[:],
+                    ya[s // per][:, s % per, 2 * u : 2 * u + 2, :].rearrange("p t j -> p (t j)"),
+                    MULT,
+                )
+                for t in (2 * u, 2 * u + 1):
+                    if s == zs - 1 and u == 1:
+                        nc.vector.tensor_scalar_add(res[:, t, :], prod[:, t, :], bias[:, t : t + 1])
+                    else:
+                        nc.scalar.activation(res[:, t, :], prod[:, t, :], IDENTITY, bias=bias[:, t : t + 1])
+                nc.sync.dma_start(
+                    out_tiles[:, 2 * u : 2 * u + 2, s * Z_SLICE : (s + 1) * Z_SLICE],
+                    res[:, 2 * u : 2 * u + 2, :],
+                )
+
+        for i in range(PACK):
+            for s in range(xs):
+                gather(xg[s][:, i, :], x_planes[i], x_list, x_wgt, s * X_SLICE, X_SLICE)
+        for s in range(xs):
+            interleave(nc.scalar.copy, xb[s][:], xg[s][:])
+        gather_z(0, W_HALF)
+        project_x(0)
+        keep_ya(0)
+        gather_z(1, W_HALF)
+        project_x(1)
+        gather_z(2, W_HALF)
+        for h in range(2):
+            interleave(nc.scalar.copy, wbb[h][:], wb_raw[h][:])
+        wq = [quantize(f"wq{h}", wbb[h], N // 2, tag="z_plane2" if h == 0 else None) for h in range(2)]
+        keep_ya(1)
+        gather_z(3, Z_SLICE)
+        for s in range(zs):
+            interleave(nc.scalar.copy, zb[s][:], zg[:, :, s * Z_SLICE : (s + 1) * Z_SLICE])
+        zq = [quantize(f"zq{s}", zb[s], Z_SLICE) for s in range(2)]
+        for s in range(zs):
+            finish(s, *zq[s])
+            if s + 2 < zs:
+                zq.append(quantize(f"zq{s + 2}", zb[s + 2], Z_SLICE))

@@ -34,6 +34,10 @@ def interleave(engine_copy, dst, src):
     )
 
 
+def interleave_pair(nc, dst, src, t0):
+    nc.scalar.copy(dst[:, :, t0 : t0 + 2], src[:, t0 : t0 + 2, :].rearrange("p t j -> p j t"))
+
+
 def tile_list_mul_bias_kernel(
     tc, xT, wgt, zT, wgt2, wa_words, wa_scales, wb, b, offs, offs2, out
 ):
@@ -59,9 +63,9 @@ def tile_list_mul_bias_kernel(
         xT_planes = xT.rearrange("(p i) t -> i p t", i=PACK)
         zT_planes = zT.rearrange("(p i) t -> i p t", i=PACK)
 
-        make_identity(nc, ident[:])
         nc.vector.memset(b_rows[:], 0.0)
         nc.vector.memset(wa_scale[:].bitcast(I32), 0)
+        make_identity(nc, ident[:])
 
         def load_scale_rows(q):
             nc.sync.dma_start(
@@ -69,6 +73,7 @@ def tile_list_mul_bias_kernel(
                 wa_scales[0, 4 * q : 4 * q + 4, :].bitcast(I32),
             )
 
+        wb_rows = wb.rearrange("(p i) n -> p i n", i=PACK)
         nc.sync.dma_start(x_planes[0][:], xT_planes[0])
         nc.sync.dma_start(x_list[:], offs)
         for h in range(2):
@@ -86,11 +91,10 @@ def tile_list_mul_bias_kernel(
         nc.sync.dma_start(z_wgt[0][:], wgt2[:, 0:W_HALF])
         nc.sync.dma_start(z_planes[0][:], zT_planes[0])
         nc.sync.dma_start(z_wgt[1][:], wgt2[:, W_HALF:J])
-        wb_rows = wb.rearrange("(p i) n -> p i n", i=PACK)
-        nc.sync.dma_start(z_planes[1][:], zT_planes[1])
         nc.sync.dma_start(wb_raw[0][:], wb_rows[:, :, 0 : N // 2])
-        nc.sync.dma_start(z_planes[2][:], zT_planes[2])
         nc.sync.dma_start(wb_raw[1][:], wb_rows[:, :, N // 2 : N])
+        nc.sync.dma_start(z_planes[1][:], zT_planes[1])
+        nc.sync.dma_start(z_planes[2][:], zT_planes[2])
         nc.sync.dma_start(z_planes[3][:], zT_planes[3])
 
         nc.tensor.transpose(banks[7][:, 0:P], b_rows[:], ident[:])
@@ -104,14 +108,16 @@ def tile_list_mul_bias_kernel(
                 MULT,
             )
 
-        def quantize(name, src, width, tag=None):
+        def quantize(codes, scale, src):
+            nc.vector.quantize_mx(
+                out=codes.bitcast(FP8X4),
+                scales=scale,
+                in_=src.rearrange("p w t -> p (w t)"),
+            )
+
+        def mx_tiles(name, width, tag=None):
             codes = keep.tile([P, width], U32, name=name + "_codes", tag=tag or name + "_codes", align_bytes=64)
             scale = keep.tile([P, width], U8, name=name + "_scale", align_bytes=64)
-            nc.vector.quantize_mx(
-                out=codes[:].bitcast(FP8X4),
-                scales=scale[:],
-                in_=src[:].rearrange("p w t -> p (w t)"),
-            )
             return codes, scale
 
         xs = J // X_SLICE
@@ -119,8 +125,11 @@ def tile_list_mul_bias_kernel(
         per = X_SLICE // Z_SLICE
         xg = [keep.tile([P, PACK, X_SLICE], F32, name=f"xg{s}") for s in range(xs)]
         xb = [keep.tile([P, X_SLICE, PACK], BF16, name=f"xb{s}", align_bytes=64) for s in range(xs)]
-        zg = keep.tile([P, PACK, J], F32, name="zg")
-        zb = [keep.tile([P, Z_SLICE, PACK], BF16, name=f"zb{s}", align_bytes=64) for s in range(zs)]
+        zg_flat = keep.tile([P, PACK * J + Z_SLICE], F32, name="zg_flat", align_bytes=64)
+        zg = zg_flat[:, 0 : PACK * J].rearrange("p (i j) -> p i j", i=PACK)
+        zb = [zg_flat[:, PACK * J - Z_SLICE :].bitcast(BF16).rearrange("p (j t) -> p j t", t=PACK)]
+        for s in range(1, zs):
+            zb.append(keep.tile([P, Z_SLICE, PACK], BF16, name=f"zb{s}", align_bytes=64)[:])
         ya = []
         wbb = [keep.tile([P, N // 2, PACK], BF16, name=f"wbb{h}", align_bytes=64) for h in range(2)]
         out_tiles = out.rearrange("(t p) j -> p t j", p=P)
@@ -130,20 +139,22 @@ def tile_list_mul_bias_kernel(
                 gather(zg[:, i, j0 : j0 + width], z_planes[i], z_list, z_wgt, j0, width)
 
         def project_x(s):
-            codes, scale = quantize(f"xq{s}", xb[s], X_SLICE, tag=f"z_plane{s}")
+            codes = xq[0][:, s * X_SLICE : (s + 1) * X_SLICE]
+            scale = xq[1][:, s * X_SLICE : (s + 1) * X_SLICE]
+            quantize(codes, scale, xb[s][:])
             for t in range(NT):
                 nc.tensor.matmul_mx(
                     out=banks[s * NT + t][:],
                     lhsT=wa_codes[:, 2 * P * t : 2 * P * (t + 1)].bitcast(FP4X4),
                     lhsT_scale=wa_scale[:, P * t : P * (t + 1)],
-                    rhs=codes[:].bitcast(FP8X4),
-                    rhs_scale=scale[:],
+                    rhs=codes.bitcast(FP8X4),
+                    rhs_scale=scale,
                     start=True,
                     stop=True,
                 )
 
         def keep_ya(s):
-            ya.append(keep.tile([P, per, NT, Z_SLICE], F32, name=f"ya{s}", tag="wb_raw1" if s else "ya0"))
+            ya.append(keep.tile([P, per, NT, Z_SLICE], F32, name=f"ya{s}", tag="ya1" if s else "wb_raw1"))
             for t in range(NT):
                 nc.scalar.copy(
                     ya[s][:, :, t, :],
@@ -173,7 +184,7 @@ def tile_list_mul_bias_kernel(
                     MULT,
                 )
                 for t in (2 * u, 2 * u + 1):
-                    if s == zs - 1 and u == 1:
+                    if (s, u) in ((0, 0), (zs - 1, 1)):
                         nc.vector.tensor_scalar_add(res[:, t, :], prod[:, t, :], bias[:, t : t + 1])
                     else:
                         nc.scalar.activation(res[:, t, :], prod[:, t, :], IDENTITY, bias=bias[:, t : t + 1])
@@ -182,26 +193,46 @@ def tile_list_mul_bias_kernel(
                     res[:, 2 * u : 2 * u + 2, :],
                 )
 
+        def z_cols(s):
+            return zg[:, :, s * Z_SLICE : (s + 1) * Z_SLICE]
+
+        def gather_last(s):
+            gather(zg[:, 3, s * Z_SLICE : (s + 1) * Z_SLICE], z_planes[3], z_list, z_wgt, s * Z_SLICE, Z_SLICE)
+
+        def quantize_wb(h):
+            interleave(nc.scalar.copy, wbb[h][:], wb_raw[h][:])
+            quantize(wq[h][0][:], wq[h][1][:], wbb[h][:])
+
+        def quantize_z(s):
+            quantize(zq[s][0][:], zq[s][1][:], zb[s])
+
+        wq = [mx_tiles(f"wq{h}", N // 2) for h in range(2)]
+        zq = [mx_tiles(f"zq{s}", Z_SLICE) for s in range(zs)]
         for i in range(PACK):
             for s in range(xs):
                 gather(xg[s][:, i, :], x_planes[i], x_list, x_wgt, s * X_SLICE, X_SLICE)
-        for s in range(xs):
-            interleave(nc.scalar.copy, xb[s][:], xg[s][:])
+                if i % 2:
+                    interleave_pair(nc, xb[s], xg[s], i - 1)
         gather_z(0, W_HALF)
+        xq = mx_tiles("xq", J, tag="z_plane0")
         project_x(0)
-        keep_ya(0)
-        gather_z(1, W_HALF)
         project_x(1)
-        gather_z(2, W_HALF)
-        for h in range(2):
-            interleave(nc.scalar.copy, wbb[h][:], wb_raw[h][:])
-        wq = [quantize(f"wq{h}", wbb[h], N // 2, tag="z_plane2" if h == 0 else None) for h in range(2)]
+        quantize_wb(0)
+        quantize_wb(1)
+        keep_ya(0)
         keep_ya(1)
-        gather_z(3, Z_SLICE)
-        for s in range(zs):
-            interleave(nc.scalar.copy, zb[s][:], zg[:, :, s * Z_SLICE : (s + 1) * Z_SLICE])
-        zq = [quantize(f"zq{s}", zb[s], Z_SLICE) for s in range(2)]
+        gather_z(1, W_HALF)
+        interleave_pair(nc, zb[0], z_cols(0), 0)
+        gather_z(2, W_HALF)
+        for s in range(3):
+            gather_last(s)
+        interleave_pair(nc, zb[0], z_cols(0), 2)
+        quantize_z(0)
+        gather_last(3)
+        for s in range(1, zs):
+            interleave(nc.scalar.copy, zb[s], z_cols(s))
+        quantize_z(1)
         for s in range(zs):
             finish(s, *zq[s])
             if s + 2 < zs:
-                zq.append(quantize(f"zq{s + 2}", zb[s + 2], Z_SLICE))
+                quantize_z(s + 2)

@@ -35,7 +35,7 @@ def interleave(engine_copy, dst, src):
 
 
 def interleave_pair(nc, dst, src, t0):
-    nc.scalar.copy(dst[:, :, t0 : t0 + 2], src[:, t0 : t0 + 2, :].rearrange("p t j -> p j t"))
+    nc.scalar.activation(dst[:, :, t0 : t0 + 2], src[:, t0 : t0 + 2, :].rearrange("p t j -> p j t"), IDENTITY)
 
 
 def tile_list_mul_bias_kernel(
@@ -54,8 +54,8 @@ def tile_list_mul_bias_kernel(
         z_wgt = [keep.tile([P, W_HALF], F32, name=f"z_wgt{h}") for h in range(2)]
         wa_codes = keep.tile([P, 2 * N], U8, name="wa_codes", align_bytes=64)
         wa_scale = keep.tile([P, N], U8, name="wa_scale", align_bytes=64)
-        wb_raw = [keep.tile([P, PACK, N // 2], F32, name=f"wb_raw{h}") for h in range(2)]
-        b_rows = keep.tile([P, P], F32, name="b_rows")
+        wb_raw = keep.tile([P, PACK, N], F32, name="wb_raw")
+        b_rows = [keep.tile([P, P], F32, name=f"b_rows{u}", align_bytes=64) for u in range(2)]
         ident = keep.tile([P, P], F32, name="ident")
         bias = keep.tile([P, NT], F32, name="bias")
         banks = [psum.tile([P, BANK], F32, name=f"bank{i}") for i in range(8)]
@@ -63,8 +63,9 @@ def tile_list_mul_bias_kernel(
         xT_planes = xT.rearrange("(p i) t -> i p t", i=PACK)
         zT_planes = zT.rearrange("(p i) t -> i p t", i=PACK)
 
-        nc.vector.memset(b_rows[:], 0.0)
         nc.vector.memset(wa_scale[:].bitcast(I32), 0)
+        for u in range(2):
+            nc.vector.memset(b_rows[u][:], 0.0)
         make_identity(nc, ident[:])
 
         def load_scale_rows(q):
@@ -73,12 +74,10 @@ def tile_list_mul_bias_kernel(
                 wa_scales[0, 4 * q : 4 * q + 4, :].bitcast(I32),
             )
 
-        wb_rows = wb.rearrange("(p i) n -> p i n", i=PACK)
         nc.sync.dma_start(x_planes[0][:], xT_planes[0])
         nc.sync.dma_start(x_list[:], offs)
         for h in range(2):
             nc.sync.dma_start(x_wgt[h][:], wgt[:, h * W_HALF : (h + 1) * W_HALF])
-        nc.sync.dma_start(b_rows[0:NT, :], b.rearrange("(t c) -> t c", c=P))
         nc.sync.dma_start(x_planes[1][:], xT_planes[1])
         load_scale_rows(0)
         load_scale_rows(1)
@@ -90,15 +89,18 @@ def tile_list_mul_bias_kernel(
         nc.sync.dma_start(z_list[:], offs2)
         nc.sync.dma_start(z_wgt[0][:], wgt2[:, 0:W_HALF])
         nc.sync.dma_start(z_planes[0][:], zT_planes[0])
+        b_tiles = b.rearrange("(t c) -> t c", c=P)
+        nc.sync.dma_start(b_rows[0][0:2, :], b_tiles[0:2, :])
         nc.sync.dma_start(z_wgt[1][:], wgt2[:, W_HALF:J])
-        nc.sync.dma_start(wb_raw[0][:], wb_rows[:, :, 0 : N // 2])
-        nc.sync.dma_start(wb_raw[1][:], wb_rows[:, :, N // 2 : N])
         nc.sync.dma_start(z_planes[1][:], zT_planes[1])
         nc.sync.dma_start(z_planes[2][:], zT_planes[2])
+        nc.sync.dma_start(wb_raw[:], wb.rearrange("(p i) n -> p i n", i=PACK))
         nc.sync.dma_start(z_planes[3][:], zT_planes[3])
+        nc.sync.dma_start(b_rows[1][0:2, :], b_tiles[2:4, :])
 
-        nc.tensor.transpose(banks[7][:, 0:P], b_rows[:], ident[:])
-        nc.scalar.activation(bias[:], banks[7][:, 0:NT], IDENTITY)
+        def spread_bias(u):
+            nc.tensor.transpose(banks[7][:, 0:P], b_rows[u][:], ident[:])
+            nc.scalar.copy(bias[:, 2 * u : 2 * u + 2], banks[7][:, 0:2])
 
         def gather(dst, plane, lst, weights, j0, width):
             nc.vector.tensor_tensor(
@@ -154,7 +156,7 @@ def tile_list_mul_bias_kernel(
                 )
 
         def keep_ya(s):
-            ya.append(keep.tile([P, per, NT, Z_SLICE], F32, name=f"ya{s}", tag="ya1" if s else "wb_raw1"))
+            ya.append(keep.tile([P, per, NT, Z_SLICE], F32, name=f"ya{s}"))
             for t in range(NT):
                 nc.scalar.copy(
                     ya[s][:, :, t, :],
@@ -184,7 +186,7 @@ def tile_list_mul_bias_kernel(
                     MULT,
                 )
                 for t in (2 * u, 2 * u + 1):
-                    if (s, u) in ((0, 0), (zs - 1, 1)):
+                    if (s, u) == (zs - 1, 1):
                         nc.vector.tensor_scalar_add(res[:, t, :], prod[:, t, :], bias[:, t : t + 1])
                     else:
                         nc.scalar.activation(res[:, t, :], prod[:, t, :], IDENTITY, bias=bias[:, t : t + 1])
@@ -199,34 +201,38 @@ def tile_list_mul_bias_kernel(
         def gather_last(s):
             gather(zg[:, 3, s * Z_SLICE : (s + 1) * Z_SLICE], z_planes[3], z_list, z_wgt, s * Z_SLICE, Z_SLICE)
 
-        def quantize_wb(h):
-            interleave(nc.scalar.copy, wbb[h][:], wb_raw[h][:])
+        def quantize_wb(h, tag=None):
+            wq.append(mx_tiles(f"wq{h}", N // 2, tag))
             quantize(wq[h][0][:], wq[h][1][:], wbb[h][:])
 
         def quantize_z(s):
             quantize(zq[s][0][:], zq[s][1][:], zb[s])
 
-        wq = [mx_tiles(f"wq{h}", N // 2) for h in range(2)]
+        wq = []
         zq = [mx_tiles(f"zq{s}", Z_SLICE) for s in range(zs)]
         for i in range(PACK):
             for s in range(xs):
                 gather(xg[s][:, i, :], x_planes[i], x_list, x_wgt, s * X_SLICE, X_SLICE)
                 if i % 2:
                     interleave_pair(nc, xb[s], xg[s], i - 1)
-        gather_z(0, W_HALF)
-        xq = mx_tiles("xq", J, tag="z_plane0")
+        gather(zg[:, 0, 0:W_HALF], z_planes[0], z_list, z_wgt, 0, W_HALF)
+        spread_bias(0)
+        xq = mx_tiles("xq", J, tag="b_rows0")
         project_x(0)
+        gather(zg[:, 0, W_HALF:J], z_planes[0], z_list, z_wgt, W_HALF, W_HALF)
         project_x(1)
-        quantize_wb(0)
-        quantize_wb(1)
         keep_ya(0)
         keep_ya(1)
         gather_z(1, W_HALF)
-        interleave_pair(nc, zb[0], z_cols(0), 0)
         gather_z(2, W_HALF)
+        for h in range(2):
+            interleave(nc.scalar.copy, wbb[h][:], wb_raw[:, :, h * (N // 2) : (h + 1) * (N // 2)])
+        quantize_wb(0)
         for s in range(3):
             gather_last(s)
-        interleave_pair(nc, zb[0], z_cols(0), 2)
+        spread_bias(1)
+        quantize_wb(1, tag="b_rows1")
+        interleave(nc.scalar.copy, zb[0], z_cols(0))
         quantize_z(0)
         gather_last(3)
         for s in range(1, zs):

@@ -15,6 +15,7 @@ U8 = mybir.dt.uint8
 FP8X4 = mybir.dt.float8_e4m3fn_x4
 FP4X4 = mybir.dt.float4_e2m1fn_x4
 MULT = mybir.AluOpType.mult
+ADD = mybir.AluOpType.add
 IDENTITY = mybir.ActivationFunctionType.Identity
 
 P = 128
@@ -56,6 +57,8 @@ def tile_list_mul_bias_kernel(
         wa_scale = keep.tile([P, N], U8, name="wa_scale", align_bytes=64)
         wb_raw = keep.tile([P, PACK, N], F32, name="wb_raw")
         b_rows = [keep.tile([P, P], F32, name=f"b_rows{u}", align_bytes=64) for u in range(2)]
+        w_rows = keep.tile([P, W_HALF], F32, name="w_rows")
+        w_cols = keep.tile([P, W_HALF], F32, name="w_cols")
         ident = keep.tile([P, P], F32, name="ident")
         bias = keep.tile([P, NT], F32, name="bias")
         banks = [psum.tile([P, BANK], F32, name=f"bank{i}") for i in range(8)]
@@ -63,6 +66,7 @@ def tile_list_mul_bias_kernel(
         xT_planes = xT.rearrange("(p i) t -> i p t", i=PACK)
         zT_planes = zT.rearrange("(p i) t -> i p t", i=PACK)
 
+        nc.vector.memset(w_rows[:], 0.0)
         nc.vector.memset(wa_scale[:].bitcast(I32), 0)
         for u in range(2):
             nc.vector.memset(b_rows[u][:], 0.0)
@@ -78,6 +82,7 @@ def tile_list_mul_bias_kernel(
         nc.sync.dma_start(x_list[:], offs)
         for h in range(2):
             nc.sync.dma_start(x_wgt[h][:], wgt[:, h * W_HALF : (h + 1) * W_HALF])
+        nc.sync.dma_start(w_rows[0:P:GROUP, :], wgt2[0:P:GROUP, 0:W_HALF])
         nc.sync.dma_start(x_planes[1][:], xT_planes[1])
         load_scale_rows(0)
         load_scale_rows(1)
@@ -87,7 +92,6 @@ def tile_list_mul_bias_kernel(
         nc.sync.dma_start(x_planes[3][:], xT_planes[3])
         nc.sync.dma_start(wa_codes[:].bitcast(I32), wa_words[0].bitcast(I32))
         nc.sync.dma_start(z_list[:], offs2)
-        nc.sync.dma_start(z_wgt[0][:], wgt2[:, 0:W_HALF])
         nc.sync.dma_start(z_planes[0][:], zT_planes[0])
         b_tiles = b.rearrange("(t c) -> t c", c=P)
         nc.sync.dma_start(b_rows[0][0:2, :], b_tiles[0:2, :])
@@ -101,6 +105,16 @@ def tile_list_mul_bias_kernel(
         def spread_bias(u):
             nc.tensor.transpose(banks[7][:, 0:P], b_rows[u][:], ident[:])
             nc.scalar.copy(bias[:, 2 * u : 2 * u + 2], banks[7][:, 0:2])
+
+        for c in range(0, W_HALF, P):
+            nc.tensor.transpose(banks[0][:, c : c + P], w_rows[:, c : c + P], ident[:])
+        nc.scalar.copy(
+            w_cols[:].rearrange("p (g r) -> p g r", r=GROUP),
+            banks[0][:].rearrange("p (g r) -> p g r", r=GROUP)[:, :, 0:1].to_broadcast([P, W_HALF // GROUP, GROUP]),
+        )
+        for c in range(0, W_HALF, P):
+            nc.tensor.transpose(banks[1][:, c : c + P], w_cols[:, c : c + P], ident[:])
+        nc.scalar.copy(z_wgt[0][:], banks[1][:])
 
         def gather(dst, plane, lst, weights, j0, width):
             nc.vector.tensor_tensor(
@@ -179,21 +193,27 @@ def tile_list_mul_bias_kernel(
                         start=True,
                         stop=True,
                     )
-                nc.vector.tensor_tensor(
-                    prod[:, 2 * u : 2 * u + 2, :].rearrange("p t j -> p (t j)"),
-                    bank[:],
-                    ya[s // per][:, s % per, 2 * u : 2 * u + 2, :].rearrange("p t j -> p (t j)"),
-                    MULT,
-                )
-                for t in (2 * u, 2 * u + 1):
-                    if (s, u) == (zs - 1, 1):
-                        nc.vector.tensor_scalar_add(res[:, t, :], prod[:, t, :], bias[:, t : t + 1])
-                    else:
-                        nc.scalar.activation(res[:, t, :], prod[:, t, :], IDENTITY, bias=bias[:, t : t + 1])
-                nc.sync.dma_start(
-                    out_tiles[:, 2 * u : 2 * u + 2, s * Z_SLICE : (s + 1) * Z_SLICE],
-                    res[:, 2 * u : 2 * u + 2, :],
-                )
+                last = (s, u) == (zs - 1, 1)
+                pieces = [(2, 3), (3, 4)] if last else [(2 * u, 2 * u + 2)]
+                for t0, t1 in pieces:
+                    nc.vector.tensor_tensor(
+                        prod[:, t0:t1, :].rearrange("p t j -> p (t j)"),
+                        bank[:, (t0 - 2 * u) * Z_SLICE : (t1 - 2 * u) * Z_SLICE],
+                        ya[s // per][:, s % per, t0:t1, :].rearrange("p t j -> p (t j)"),
+                        MULT,
+                    )
+                for t0, t1 in pieces:
+                    for t in range(t0, t1):
+                        if last and t == NT - 1:
+                            nc.vector.tensor_scalar_add(res[:, t, :], prod[:, t, :], bias[:, t : t + 1])
+                        elif s == 0:
+                            nc.gpsimd.tensor_scalar(res[:, t, :], prod[:, t, :], 1.0, bias[:, t : t + 1], MULT, ADD)
+                        else:
+                            nc.scalar.activation(res[:, t, :], prod[:, t, :], IDENTITY, bias=bias[:, t : t + 1])
+                    nc.sync.dma_start(
+                        out_tiles[:, t0:t1, s * Z_SLICE : (s + 1) * Z_SLICE],
+                        res[:, t0:t1, :],
+                    )
 
         def z_cols(s):
             return zg[:, :, s * Z_SLICE : (s + 1) * Z_SLICE]

from contextlib import ExitStack

import concourse.mybir as mybir
from concourse.masks import make_identity

K, L, N, T, J = 512, 512, 512, 2048, 1024
FLOPS = 2 * (K + L) * N * J

F32 = mybir.dt.float32
BF16 = mybir.dt.bfloat16
I32 = mybir.dt.int32
U32 = mybir.dt.uint32
U16 = mybir.dt.uint16
U8 = mybir.dt.uint8
FP8X4 = mybir.dt.float8_e4m3fn_x4
FP4X4 = mybir.dt.float4_e2m1fn_x4
MULT = mybir.AluOpType.mult
ADD = mybir.AluOpType.add
IDENTITY = mybir.ActivationFunctionType.Identity

P = 128
PACK = 4
GROUP = 16
NT = N // P
BANK = 512
X_SLICE = 512
Z_SLICE = 256
W_HALF = J // 2


def interleave(engine_copy, dst, src):
    engine_copy(
        dst.rearrange("p (c i) t -> p c t i", i=4),
        src.rearrange("p t (c i) -> p c t i", i=4),
    )


def interleave_pair(nc, dst, src, t0):
    nc.scalar.activation(dst[:, :, t0 : t0 + 2], src[:, t0 : t0 + 2, :].rearrange("p t j -> p j t"), IDENTITY)


def tile_list_mul_bias_kernel(
    tc, xT, wgt, zT, wgt2, wa_words, wa_scales, wb, b, offs, offs2, out
):
    nc = tc.nc
    with ExitStack() as ctx:
        keep = ctx.enter_context(tc.tile_pool(name="keep", bufs=1))
        psum = ctx.enter_context(tc.psum_pool(name="psum", bufs=1))

        x_list = keep.tile([P, J // GROUP], U16, name="x_list")
        z_list = keep.tile([P, J // GROUP], U16, name="z_list")
        x_planes = [keep.tile([P, T], F32, name=f"x_plane{i}") for i in range(PACK)]
        z_planes = [keep.tile([P, T], F32, name=f"z_plane{i}", align_bytes=64) for i in range(PACK)]
        x_wgt = [keep.tile([P, W_HALF], F32, name=f"x_wgt{h}") for h in range(2)]
        z_wgt = [keep.tile([P, W_HALF], F32, name=f"z_wgt{h}") for h in range(2)]
        wa_codes = keep.tile([P, 2 * N], U8, name="wa_codes", align_bytes=64)
        wa_scale = keep.tile([P, N], U8, name="wa_scale", align_bytes=64)
        wb_raw = keep.tile([P, PACK, N], F32, name="wb_raw")
        b_rows = [keep.tile([P, P], F32, name=f"b_rows{u}", align_bytes=64) for u in range(2)]
        w_rows = keep.tile([P, W_HALF], F32, name="w_rows")
        w_cols = keep.tile([P, W_HALF], F32, name="w_cols")
        ident = keep.tile([P, P], F32, name="ident")
        bias = keep.tile([P, NT], F32, name="bias")
        banks = [psum.tile([P, BANK], F32, name=f"bank{i}") for i in range(8)]

        xT_planes = xT.rearrange("(p i) t -> i p t", i=PACK)
        zT_planes = zT.rearrange("(p i) t -> i p t", i=PACK)

        nc.vector.memset(w_rows[:], 0.0)
        nc.vector.memset(wa_scale[:].bitcast(I32), 0)
        for u in range(2):
            nc.vector.memset(b_rows[u][:], 0.0)
        make_identity(nc, ident[:])

        def load_scale_rows(q):
            nc.sync.dma_start(
                wa_scale[32 * q : 32 * q + 4, :].bitcast(I32),
                wa_scales[0, 4 * q : 4 * q + 4, :].bitcast(I32),
            )

        nc.sync.dma_start(x_planes[0][:], xT_planes[0])
        nc.sync.dma_start(x_list[:], offs)
        for h in range(2):
            nc.sync.dma_start(x_wgt[h][:], wgt[:, h * W_HALF : (h + 1) * W_HALF])
        nc.sync.dma_start(w_rows[0:P:GROUP, :], wgt2[0:P:GROUP, 0:W_HALF])
        nc.sync.dma_start(x_planes[1][:], xT_planes[1])
        load_scale_rows(0)
        load_scale_rows(1)
        nc.sync.dma_start(x_planes[2][:], xT_planes[2])
        load_scale_rows(2)
        load_scale_rows(3)
        nc.sync.dma_start(x_planes[3][:], xT_planes[3])
        nc.sync.dma_start(wa_codes[:].bitcast(I32), wa_words[0].bitcast(I32))
        nc.sync.dma_start(z_list[:], offs2)
        nc.sync.dma_start(z_planes[0][:], zT_planes[0])
        b_tiles = b.rearrange("(t c) -> t c", c=P)
        nc.sync.dma_start(b_rows[0][0:2, :], b_tiles[0:2, :])
        nc.sync.dma_start(z_wgt[1][:], wgt2[:, W_HALF:J])
        nc.sync.dma_start(z_planes[1][:], zT_planes[1])
        nc.sync.dma_start(z_planes[2][:], zT_planes[2])
        nc.sync.dma_start(wb_raw[:], wb.rearrange("(p i) n -> p i n", i=PACK))
        nc.sync.dma_start(z_planes[3][:], zT_planes[3])
        nc.sync.dma_start(b_rows[1][0:2, :], b_tiles[2:4, :])

        def spread_bias(u):
            nc.tensor.transpose(banks[7][:, 0:P], b_rows[u][:], ident[:])
            nc.scalar.copy(bias[:, 2 * u : 2 * u + 2], banks[7][:, 0:2])

        for c in range(0, W_HALF, P):
            nc.tensor.transpose(banks[0][:, c : c + P], w_rows[:, c : c + P], ident[:])
        nc.scalar.copy(
            w_cols[:].rearrange("p (g r) -> p g r", r=GROUP),
            banks[0][:].rearrange("p (g r) -> p g r", r=GROUP)[:, :, 0:1].to_broadcast([P, W_HALF // GROUP, GROUP]),
        )
        for c in range(0, W_HALF, P):
            nc.tensor.transpose(banks[1][:, c : c + P], w_cols[:, c : c + P], ident[:])
        nc.scalar.copy(z_wgt[0][:], banks[1][:])

        def gather(dst, plane, lst, weights, j0, width):
            nc.vector.tensor_tensor(
                dst,
                plane[:].indirect(lst[:, j0 // GROUP : (j0 + width) // GROUP]),
                weights[j0 // W_HALF][:, j0 % W_HALF : j0 % W_HALF + width],
                MULT,
            )

        def quantize(codes, scale, src):
            nc.vector.quantize_mx(
                out=codes.bitcast(FP8X4),
                scales=scale,
                in_=src.rearrange("p w t -> p (w t)"),
            )

        def mx_tiles(name, width, tag=None):
            codes = keep.tile([P, width], U32, name=name + "_codes", tag=tag or name + "_codes", align_bytes=64)
            scale = keep.tile([P, width], U8, name=name + "_scale", align_bytes=64)
            return codes, scale

        xs = J // X_SLICE
        zs = J // Z_SLICE
        per = X_SLICE // Z_SLICE
        xg = [keep.tile([P, PACK, X_SLICE], F32, name=f"xg{s}") for s in range(xs)]
        xb = [keep.tile([P, X_SLICE, PACK], BF16, name=f"xb{s}", align_bytes=64) for s in range(xs)]
        zg_flat = keep.tile([P, PACK * J + Z_SLICE], F32, name="zg_flat", align_bytes=64)
        zg = zg_flat[:, 0 : PACK * J].rearrange("p (i j) -> p i j", i=PACK)
        zb = [zg_flat[:, PACK * J - Z_SLICE :].bitcast(BF16).rearrange("p (j t) -> p j t", t=PACK)]
        for s in range(1, zs):
            zb.append(keep.tile([P, Z_SLICE, PACK], BF16, name=f"zb{s}", align_bytes=64)[:])
        ya = []
        wbb = [keep.tile([P, N // 2, PACK], BF16, name=f"wbb{h}", align_bytes=64) for h in range(2)]
        out_tiles = out.rearrange("(t p) j -> p t j", p=P)

        def gather_z(i, width):
            for j0 in range(0, J, width):
                gather(zg[:, i, j0 : j0 + width], z_planes[i], z_list, z_wgt, j0, width)

        def project_x(s):
            codes = xq[0][:, s * X_SLICE : (s + 1) * X_SLICE]
            scale = xq[1][:, s * X_SLICE : (s + 1) * X_SLICE]
            quantize(codes, scale, xb[s][:])
            for t in range(NT):
                nc.tensor.matmul_mx(
                    out=banks[s * NT + t][:],
                    lhsT=wa_codes[:, 2 * P * t : 2 * P * (t + 1)].bitcast(FP4X4),
                    lhsT_scale=wa_scale[:, P * t : P * (t + 1)],
                    rhs=codes.bitcast(FP8X4),
                    rhs_scale=scale,
                    start=True,
                    stop=True,
                )

        def keep_ya(s):
            ya.append(keep.tile([P, per, NT, Z_SLICE], F32, name=f"ya{s}"))
            for t in range(NT):
                nc.scalar.copy(
                    ya[s][:, :, t, :],
                    banks[s * NT + t][:].rearrange("p (s j) -> p s j", s=per),
                )

        def finish(s, codes, scale):
            prod = keep.tile([P, NT, Z_SLICE], F32, name=f"prod{s}")
            res = keep.tile([P, NT, Z_SLICE], F32, name=f"res{s}")
            for u in range(NT // 2):
                bank = banks[2 * s + u]
                for v in range(2):
                    t = 2 * u + v
                    nc.tensor.matmul_mx(
                        out=bank[:, v * Z_SLICE : (v + 1) * Z_SLICE],
                        lhsT=wq[u][0][:, P * v : P * (v + 1)].bitcast(FP8X4),
                        lhsT_scale=wq[u][1][:, P * v : P * (v + 1)],
                        rhs=codes[:].bitcast(FP8X4),
                        rhs_scale=scale[:],
                        start=True,
                        stop=True,
                    )
                last = (s, u) == (zs - 1, 1)
                pieces = [(2, 3), (3, 4)] if last else [(2 * u, 2 * u + 2)]
                for t0, t1 in pieces:
                    nc.vector.tensor_tensor(
                        prod[:, t0:t1, :].rearrange("p t j -> p (t j)"),
                        bank[:, (t0 - 2 * u) * Z_SLICE : (t1 - 2 * u) * Z_SLICE],
                        ya[s // per][:, s % per, t0:t1, :].rearrange("p t j -> p (t j)"),
                        MULT,
                    )
                for t0, t1 in pieces:
                    for t in range(t0, t1):
                        if last and t == NT - 1:
                            nc.vector.tensor_scalar_add(res[:, t, :], prod[:, t, :], bias[:, t : t + 1])
                        elif s == 0:
                            nc.gpsimd.tensor_scalar(res[:, t, :], prod[:, t, :], 1.0, bias[:, t : t + 1], MULT, ADD)
                        else:
                            nc.scalar.activation(res[:, t, :], prod[:, t, :], IDENTITY, bias=bias[:, t : t + 1])
                    nc.sync.dma_start(
                        out_tiles[:, t0:t1, s * Z_SLICE : (s + 1) * Z_SLICE],
                        res[:, t0:t1, :],
                    )

        def z_cols(s):
            return zg[:, :, s * Z_SLICE : (s + 1) * Z_SLICE]

        def gather_last(s):
            gather(zg[:, 3, s * Z_SLICE : (s + 1) * Z_SLICE], z_planes[3], z_list, z_wgt, s * Z_SLICE, Z_SLICE)

        def quantize_wb(h, tag=None):
            wq.append(mx_tiles(f"wq{h}", N // 2, tag))
            quantize(wq[h][0][:], wq[h][1][:], wbb[h][:])

        def quantize_z(s):
            quantize(zq[s][0][:], zq[s][1][:], zb[s])

        wq = []
        zq = [mx_tiles(f"zq{s}", Z_SLICE) for s in range(zs)]
        for i in range(PACK):
            for s in range(xs):
                gather(xg[s][:, i, :], x_planes[i], x_list, x_wgt, s * X_SLICE, X_SLICE)
                if i % 2:
                    interleave_pair(nc, xb[s], xg[s], i - 1)
        gather(zg[:, 0, 0:W_HALF], z_planes[0], z_list, z_wgt, 0, W_HALF)
        spread_bias(0)
        xq = mx_tiles("xq", J, tag="b_rows0")
        project_x(0)
        gather(zg[:, 0, W_HALF:J], z_planes[0], z_list, z_wgt, W_HALF, W_HALF)
        project_x(1)
        keep_ya(0)
        keep_ya(1)
        gather_z(1, W_HALF)
        gather_z(2, W_HALF)
        for h in range(2):
            interleave(nc.scalar.copy, wbb[h][:], wb_raw[:, :, h * (N // 2) : (h + 1) * (N // 2)])
        quantize_wb(0)
        for s in range(3):
            gather_last(s)
        spread_bias(1)
        quantize_wb(1, tag="b_rows1")
        interleave(nc.scalar.copy, zb[0], z_cols(0))
        quantize_z(0)
        gather_last(3)
        for s in range(1, zs):
            interleave(nc.scalar.copy, zb[s], z_cols(s))
        quantize_z(1)
        for s in range(zs):
            finish(s, *zq[s])
            if s + 2 < zs:
                quantize_z(s + 2)
